import numpy as np
import ml_dtypes


def mxq(x, axis, fmt="e4m3"):
    dtype, down = {"e4m3": (ml_dtypes.float8_e4m3fn, 7), "e5m2": (ml_dtypes.float8_e5m2, 14)}[fmt]
    v = np.moveaxis(np.asarray(x, np.float32).astype(ml_dtypes.bfloat16).astype(np.float64), axis, -1)
    blocks = v.reshape(v.shape[:-1] + (-1, 32))
    amax = np.abs(blocks).max(-1, keepdims=True)
    byte = np.maximum(np.where(amax > 0, np.frexp(amax)[1] - 1 + 127, 0) - down, 1)
    scale = np.exp2(byte - 127.0)
    codes = (blocks / scale).astype(np.float32).astype(dtype).astype(np.float64)
    return np.moveaxis((codes * scale).reshape(v.shape), -1, axis)


WIDE = False


def mx_kscale(k):
    if not WIDE:
        return np.ones(k)
    levels = np.array([10, -10, 5, -5, 0])
    if k % 512:
        return np.exp2(np.random.permutation(np.resize(levels, k // 32))).repeat(32)
    a = np.empty((k // 512, 16))
    for p in range(k // 512):
        a[p, :8] = np.random.permutation(np.resize(levels, 8))
        for g in range(8):
            far = levels[np.abs(levels - a[p, g]) >= 10]
            a[p, g + 8] = far[np.random.randint(len(far))]
    return np.exp2(a.ravel()).repeat(32)


def f64(x):
    return np.asarray(x).astype(np.float64)


def striped(idx):
    return np.tile(idx.reshape(-1, 16).T, (8, 1)).astype(np.uint16)


def unstriped(offs):
    return offs[:16].T.reshape(-1).astype(np.int64)


def striped8(idx):
    return np.concatenate([x.reshape(-1, 16).T for x in idx]).astype(np.uint16)


def runs(offs, k):
    lists = np.stack([offs[16 * r : 16 * r + 16].T.reshape(-1) for r in range(8)]).astype(np.int64)
    return lists[np.arange(k) % 512 // 64]


def pack_weight(w):
    k, n = w.shape
    w = f64(np.asarray(w, np.float32).astype(ml_dtypes.bfloat16)).reshape(k // 32, 32, n)
    amax = np.abs(w).max(1)
    byte = np.clip(np.where(amax > 0, np.frexp(amax)[1] - 1 + 127 - 7, 1), 1, 254)
    scaled = (w * np.exp2(127.0 - byte)[:, None, :]).reshape(k, n).astype(np.float32)
    words = np.ascontiguousarray(scaled.reshape(k // 512, 128, 4, n).transpose(0, 1, 3, 2)).astype(ml_dtypes.float8_e4m3fn).view(np.uint8)
    return words, np.ascontiguousarray(byte.astype(np.uint8).reshape(k // 512, 16, n))


def unpack_weight(words, scales):
    g, p, n, _ = words.shape
    vals = np.ascontiguousarray(words).view(ml_dtypes.float8_e4m3fn).astype(np.float64) * np.repeat(np.exp2(scales.astype(np.float64) - 127.0), 8, axis=1)[..., None]
    return vals.transpose(0, 1, 3, 2).reshape(g * 512, n)


E2M1 = np.array([0.0, 0.5, 1.0, 1.5, 2.0, 3.0, 4.0, 6.0, -0.0, -0.5, -1.0, -1.5, -2.0, -3.0, -4.0, -6.0])


def pack_fp4(w):
    k, n = w.shape
    w = f64(np.asarray(w, np.float32).astype(ml_dtypes.bfloat16)).reshape(k // 32, 32, n)
    amax = np.abs(w).max(1)
    mant, ex = np.frexp(amax / 6.0)
    byte = np.clip(np.where(amax > 0, np.where(mant > 0.5, ex, ex - 1) + 127, 1), 1, 254)
    scaled = (w * np.exp2(127.0 - byte)[:, None, :]).reshape(k, n).astype(np.float32)
    c = np.ascontiguousarray(scaled.reshape(k // 512, 128, 4, n).transpose(0, 1, 3, 2)).astype(ml_dtypes.float4_e2m1fn).view(np.uint8) & 0xF
    words = (c[..., 0::2] | (c[..., 1::2] << 4)).reshape(k // 512, 128, 2 * n)
    return np.ascontiguousarray(words), np.ascontiguousarray(byte.astype(np.uint8).reshape(k // 512, 16, n))


def unpack_fp4(words, scales):
    g, _, n = scales.shape
    words = np.ascontiguousarray(words).reshape(g, 128, n, 2)
    nib = np.empty((g, 128, n, 4), np.uint8)
    nib[..., 0::2] = words & 0xF
    nib[..., 1::2] = words >> 4
    vals = E2M1[nib] * np.repeat(np.exp2(scales.astype(np.float64) - 127.0), 8, axis=1)[..., None]
    return vals.transpose(0, 1, 3, 2).reshape(g * 512, n)


def planes(y):
    n, m = y.shape
    v = y.astype(np.float32).astype(ml_dtypes.bfloat16).astype(np.float64).reshape(n // 32, 32, m)
    top = np.abs(v).max(1)
    byte = np.clip(np.where(top > 0, np.frexp(top)[1] - 1 + 127 - 7, 1), 1, 254)
    codes = (v * np.exp2(127.0 - byte)[:, None, :]).reshape(n, m).astype(np.float32).astype(ml_dtypes.float8_e4m3fn).view(np.uint8)
    words = codes.reshape(n // 512, 128, 4, m).transpose(0, 1, 3, 2)
    return np.ascontiguousarray(words), np.ascontiguousarray(byte.astype(np.uint8).reshape(n // 512, 16, m))


K, T, S, N, H, G, W = 512, 1024, 512, 512, 512, 2048, 384


def setup_inputs():
    n = np.random.standard_normal
    s = mx_kscale(K)[:, None]
    u = mx_kscale(S)
    packed_xT = pack_weight(n((K, T)) * s)
    packed_w1 = pack_fp4(n((K, H)) / np.sqrt(K) / s)
    packed_dT = pack_weight(n((K, G)) / s)
    packed_w2 = pack_fp4(n((H, N)) / np.sqrt(2 * H) / u[:, None])
    packed_w3 = pack_fp4(n((H, N)) / np.sqrt(2 * H) / u[:, None])
    return {
        "x_words": packed_xT[0],
        "x_scales": packed_xT[1],
        "w1_words": packed_w1[0],
        "w1_scales": packed_w1[1],
        "d_words": packed_dT[0],
        "d_scales": packed_dT[1],
        "gn": (np.random.uniform(0.5, 1.5, (H, 1)) * u[:, None]).astype(np.float32),
        "gk": (np.random.uniform(0.5, 1.5, (H, 1)) * u[:, None]).astype(np.float32),
        "w2_words": packed_w2[0],
        "w2_scales": packed_w2[1],
        "w3_words": packed_w3[0],
        "w3_scales": packed_w3[1],
        "offs": striped(np.random.permutation(T)[:S]),
        "kidx": striped8(np.random.randint(0, G, (8, H))),
        "two": striped(np.random.permutation(T)[:S]),
        "n1": striped(np.random.permutation(S)[:W]),
        "n2": striped(np.random.permutation(S)[:W]),
        "n3": striped(np.random.permutation(S)[:W]),
        "n4": striped(np.random.permutation(S)[:W]),
        "n5": striped8(np.stack([np.random.permutation(S) for _ in range(8)])),
        "n6": striped8(np.stack([np.random.permutation(S) for _ in range(8)])),
    }


def reference(x_words, x_scales, w1_words, w1_scales, d_words, d_scales, gn, gk, w2_words, w2_scales, w3_words, w3_scales, offs, kidx, two, n1, n2, n3, n4, n5, n6):
    xq = unpack_weight(x_words, x_scales)[:, unstriped(offs)]
    y = unpack_fp4(w1_words, w1_scales).T @ xq
    old = y[:, unstriped(n1)]
    pa = y[:, unstriped(n2)]
    ra = old - (0.5 * pa)
    ds = y.copy()
    ds[:, unstriped(n1)] = ra
    z = f64(gn) * ds
    d_kidx = unpack_weight(d_words, d_scales)[np.arange(K)[:, None], runs(kidx, K)]
    x_two = unpack_weight(x_words, x_scales)[:, unstriped(two)]
    s = 0.0625 * (d_kidx.T @ x_two)
    old2 = s[:, unstriped(n3)]
    pa2 = s[:, unstriped(n4)]
    ra2 = old2 / (np.abs(pa2) + 0.5)
    ds2 = s.copy()
    ds2[:, unstriped(n3)] = ra2
    z2 = f64(gk) * ds2
    h = unpack_fp4(w2_words, w2_scales).T @ mxq(z, 0, "e4m3") + unpack_fp4(w3_words, w3_scales).T @ mxq(z2, 0, "e4m3")
    out_0 = (np.tanh(h[np.arange(N)[:, None], runs(n5, N)] - h)) * (h[np.arange(N)[:, None], runs(n6, N)])
    return (out_0,) + planes(out_0)

@@ -1,0 +1,255 @@
+from contextlib import ExitStack
+
+import concourse.mybir as mybir
+
+F32 = mybir.dt.float32
+BF16 = mybir.dt.bfloat16
+I32 = mybir.dt.int32
+U32 = mybir.dt.uint32
+U16 = mybir.dt.uint16
+U8 = mybir.dt.uint8
+FP8X4 = mybir.dt.float8_e4m3fn_x4
+FP4X4 = mybir.dt.float4_e2m1fn_x4
+ACT = mybir.ActivationFunctionType
+ALU = mybir.AluOpType
+
+P = 128
+S = 512
+W = 384
+FLOPS = 4 * 2 * 512 * 512 * 512
+
+
+def tile_picked_jkeykdifknormfdif_none_po_kernel(
+    tc, x_words, x_scales, w1_words, w1_scales, d_words, d_scales, gn, gk, w2_words, w2_scales,
+    w3_words, w3_scales, offs, kidx, two, n1, n2, n3, n4, n5, n6, out_0, out_1, out_2,
+):
+    nc = tc.nc
+    with ExitStack() as ctx:
+        lists = ctx.enter_context(tc.tile_pool(name="lists", bufs=1))
+        sb = ctx.enter_context(tc.tile_pool(name="sb", bufs=1))
+        psum = ctx.enter_context(tc.psum_pool(name="psum", bufs=1))
+
+        def load_list(src, name):
+            tile = lists.tile([P, src.shape[1]], U16, name=name)
+            nc.sync.dma_start(tile[:], src)
+            return tile
+
+        def zeroed_bytes(width, name):
+            tile = sb.tile([P, width], U8, name=name, align_bytes=64)
+            nc.vector.memset(tile[:].bitcast(I32), 0)
+            return tile
+
+        def load_scale_rows(tile, src):
+            for q in range(4):
+                nc.sync.dma_start(out=tile[32 * q : 32 * q + 4, :].bitcast(I32), in_=src[0, 4 * q : 4 * q + 4, :].bitcast(I32))
+
+        def load_words(src, name):
+            tile = sb.tile([P, src.shape[2]], I32, name=name, align_bytes=64)
+            nc.sync.dma_start(out=tile[:], in_=src[0].rearrange("p n t -> p (n t)").bitcast(I32))
+            return tile
+
+        def load_fp4(src, name):
+            tile = sb.tile([P, 2 * S], U8, name=name, tag="fp4_raw", align_bytes=64)
+            nc.sync.dma_start(out=tile[:].bitcast(I32), in_=src[0].bitcast(I32))
+            return tile
+
+        def load_gain(src, name):
+            tile = sb.tile([P, 4], F32, name=name)
+            nc.sync.dma_start(out=tile[:], in_=src.rearrange("(p t) o -> p (t o)", t=4))
+            return tile
+
+        def deal(src, dtype, width, name, tag=None, engine=nc.vector):
+            tile = sb.tile([P, S * width], dtype, name=name, tag=tag or name, align_bytes=64)
+            engine.tensor_copy(
+                out=tile[:].rearrange("p (t m b) -> p t m b", t=4, b=width),
+                in_=src.rearrange("p (m t b) -> p t m b", t=4, b=width),
+            )
+            return tile
+
+        def gather_codes(table, offsets, dtype, name):
+            tile = sb.tile([P, S], dtype, name=name, align_bytes=64)
+            nc.vector.tensor_copy(tile[:], table[:].bitcast(dtype).indirect(offsets[:]))
+            return tile
+
+        def gather_bytes(table, offsets, name):
+            tile = sb.tile([P, S], U8, name=name, align_bytes=64)
+            nc.vector.tensor_copy(tile[:], table[:].indirect(offsets[:]))
+            return tile
+
+        def weave(copy, planes, name):
+            woven = sb.tile([P, planes.shape[2], 4], BF16, name=name + "_woven", align_bytes=64)
+            copy(woven[:].rearrange("p (c i) t -> p c t i", i=4), planes[:].rearrange("p t (c i) -> p c t i", i=4))
+            return woven
+
+        def quantize(planes, name):
+            woven = weave(nc.vector.tensor_copy, planes, name)
+            codes = sb.tile([P, S], I32, name=name + "_codes", align_bytes=64)
+            scales = sb.tile([P, S], U8, name=name + "_scales", align_bytes=64)
+            nc.vector.quantize_mx(out=codes[:].bitcast(FP8X4), scales=scales[:], in_=woven[:].rearrange("p j t -> p (j t)"))
+            return codes, scales
+
+        xs_table = zeroed_bytes(1024, "xs_table")
+        w1s_raw = zeroed_bytes(S, "w1s_raw")
+        ds_table = zeroed_bytes(2048, "ds_table")
+        ds_final = zeroed_bytes(S, "ds_final")
+        w2s_raw = zeroed_bytes(S, "w2s_raw")
+        w3s_raw = zeroed_bytes(S, "w3s_raw")
+        half = sb.tile([P, 1], F32, name="half")
+        nc.vector.memset(half[:], 0.5)
+
+        w1w_raw = load_fp4(w1_words, "w1w_raw")
+        offs_t = load_list(offs, "offs_t")
+        xw_table = load_words(x_words, "xw_table")
+        load_scale_rows(xs_table, x_scales)
+        load_scale_rows(w1s_raw, w1_scales)
+        kidx_t = load_list(kidx, "kidx_t")
+        nc.sync.dma_start(out=ds_table[0:P:8, :].bitcast(I32), in_=d_scales[0].bitcast(I32))
+        n2_t = load_list(n2, "n2_t")
+        dw_table = load_words(d_words, "dw_table")
+        two_t = load_list(two, "two_t")
+        n1_t = load_list(n1, "n1_t")
+        n4_t = load_list(n4, "n4_t")
+        n3_t = load_list(n3, "n3_t")
+        gn_t = load_gain(gn, "gn_t")
+        gk_t = load_gain(gk, "gk_t")
+
+        xq_scales = gather_bytes(xs_table, offs_t, "xq_scales")
+        xq_words = gather_codes(xw_table, offs_t, U32, "xq_words")
+        w1w = deal(w1w_raw[:], U8, 2, "w1w")
+        w1s = deal(w1s_raw[:], U8, 1, "w1s")
+
+        y_acc = [psum.tile([P, S], F32, name=f"y_acc{t}", tag=f"bank_a{t}") for t in range(4)]
+        for t in range(4):
+            nc.tensor.matmul_mx(
+                out=y_acc[t][:], lhsT=w1w[:, 256 * t : 256 * (t + 1)].bitcast(FP4X4), lhsT_scale=w1s[:, P * t : P * (t + 1)],
+                rhs=xq_words[:].bitcast(FP8X4), rhs_scale=xq_scales[:], start=True, stop=True,
+            )
+
+        dq_scales = gather_bytes(ds_table, kidx_t, "dq_scales")
+        dq_scales_dealt = deal(dq_scales[:], U8, 1, "dq_scales_dealt")
+        for q in range(4):
+            nc.sync.dma_start(
+                out=ds_final[32 * q : 32 * q + 4, :].bitcast(I32),
+                in_=dq_scales_dealt[32 * q : 32 * (q + 1) : 8, :].bitcast(I32),
+            )
+        dq_words = gather_codes(dw_table, kidx_t, U32, "dq_words")
+        dq_words_dealt = deal(dq_words[:].bitcast(I32), I32, 1, "dq_words_dealt", "keys_then_ra")
+        x2_scales = gather_bytes(xs_table, two_t, "x2_scales")
+        x2_words = gather_codes(xw_table, two_t, U32, "x2_words")
+
+        s_acc = [psum.tile([P, S], F32, name=f"s_acc{t}", tag=f"bank_b{t}") for t in range(4)]
+        for t in range(4):
+            nc.tensor.matmul_mx(
+                out=s_acc[t][:], lhsT=dq_words_dealt[:, P * t : P * (t + 1)].bitcast(FP8X4), lhsT_scale=ds_final[:, P * t : P * (t + 1)],
+                rhs=x2_words[:].bitcast(FP8X4), rhs_scale=x2_scales[:], start=True, stop=True,
+            )
+
+        w2w_raw = load_fp4(w2_words, "w2w_raw")
+        load_scale_rows(w2s_raw, w2_scales)
+        load_scale_rows(w3s_raw, w3_scales)
+        n5_t = load_list(n5, "n5_t")
+        n6_t = load_list(n6, "n6_t")
+
+        ys = [sb.tile([P, S], F32, name=f"y{t}") for t in range(4)]
+        lesses = []
+        for t in range(4):
+            (nc.vector.tensor_copy if t in [] else nc.scalar.copy)(ys[t][:], y_acc[t][:])
+            less = sb.tile([P, W], F32, name=f"less{t}")
+            nc.scalar.activation(less[:], ys[t][:].indirect(n2_t[:]), ACT.Copy, scale=-0.5)
+            lesses.append(less)
+
+        w2w = deal(w2w_raw[:], U8, 2, "w2w")
+        w3w_raw = load_fp4(w3_words, "w3w_raw")
+        w2s = deal(w2s_raw[:], U8, 1, "w2s")
+        w3s = deal(w3s_raw[:], U8, 1, "w3s")
+        ra = sb.tile([P, 4, W], F32, name="ra", tag="keys_then_ra", align_bytes=64)
+        for t in range(4):
+            nc.vector.tensor_tensor(ra[:, t, :], ys[t][:].indirect(n1_t[:]), lesses[t][:], ALU.add)
+        w3w = deal(w3w_raw[:], U8, 2, "w3w")
+        gk16 = sb.tile([P, 4], F32, name="gk16")
+        nc.vector.tensor_scalar(gk16[:], gk_t[:], 0.0625, None, ALU.mult)
+
+        z_planes = sb.tile([P, 4, S], BF16, name="z_planes")
+        z2_planes = sb.tile([P, 4, S], BF16, name="z2_planes")
+        late = []
+
+        def rounded(planes, tiles, gain, t, on_scalar):
+            if t in on_scalar:
+                nc.scalar.activation(planes[:, t, :], tiles[t][:], ACT.Copy, scale=gain[:, t : t + 1])
+            else:
+                nc.vector.tensor_scalar(planes[:, t, :], tiles[t][:], gain[:, t : t + 1], None, ALU.mult)
+
+        ss = [sb.tile([P, S], F32, name=f"s{t}") for t in range(4)]
+        for t in range(4):
+            (nc.vector.tensor_copy if t in [] else nc.scalar.copy)(ss[t][:], s_acc[t][:])
+            pa2 = sb.tile([P, W], F32, name=f"pa2_{t}")
+            nc.scalar.activation(pa2[:], ss[t][:].indirect(n4_t[:]), ACT.Copy)
+            size = sb.tile([P, W], F32, name=f"size{t}")
+            nc.scalar.activation(size[:], pa2[:], ACT.Abs, scale=0.0625)
+            root = sb.tile([P, W], F32, name=f"root{t}")
+            nc.scalar.activation(root[:], size[:], ACT.Abs_reciprocal_sqrt, bias=half[:])
+            once = sb.tile([P, W], F32, name=f"once{t}")
+            nc.vector.tensor_tensor(once[:], ss[t][:].indirect(n3_t[:]), root[:], ALU.mult)
+            if t in []:
+                twice = sb.tile([P, W], F32, name=f"twice{t}")
+                nc.vector.tensor_tensor(twice[:], once[:], root[:], ALU.mult)
+                late.append((t, twice))
+            else:
+                nc.vector.tensor_tensor(ss[t][:].indirect(n3_t[:]), once[:], root[:], ALU.mult)
+                rounded(z2_planes, ss, gk16, t, [])
+        for t, twice in late:
+            nc.scalar.activation(ss[t][:].indirect(n3_t[:]), twice[:], ACT.Copy)
+            rounded(z2_planes, ss, gk16, t, [])
+        z2_codes, z2_scales = quantize(z2_planes, "z2")
+        for t in range(4):
+            nc.scalar.activation(ys[t][:].indirect(n1_t[:]), ra[:, t, :], ACT.Copy)
+            rounded(z_planes, ys, gn_t, t, [])
+        z_codes, z_scales = quantize(z_planes, "z")
+
+        h_acc = [psum.tile([P, S], F32, name=f"h_acc{t}", tag=f"bank_a{t}") for t in range(4)]
+        for first, ww, ws, codes, scales in ((True, w3w, w3s, z2_codes, z2_scales), (False, w2w, w2s, z_codes, z_scales)):
+            for t in range(4):
+                nc.tensor.matmul_mx(
+                    out=h_acc[t][:], lhsT=ww[:, 256 * t : 256 * (t + 1)].bitcast(FP4X4), lhsT_scale=ws[:, P * t : P * (t + 1)],
+                    rhs=codes[:].bitcast(FP8X4), rhs_scale=scales[:], start=first, stop=not first,
+                )
+
+        hs = [sb.tile([P, S], F32, name=f"h{t}") for t in range(4)]
+        for t in range(4):
+            (nc.scalar.copy if t in [0] else nc.vector.tensor_copy)(hs[t][:], h_acc[t][:])
+        out_rows = out_0.rearrange("(p t) j -> p t j", t=4)
+        out_words = out_1[0].rearrange("p n t -> p (n t)").bitcast(I32)
+        o_codes = sb.tile([P, S], I32, name="o_codes", align_bytes=64)
+        o_scales = sb.tile([P, S], U8, name="o_scales", align_bytes=64)
+        start = 0
+        finish = []
+        for c, width in enumerate([256,256]):
+            cols = slice(start, start + width)
+            entries = slice(start // 16, (start + width) // 16)
+            start = start + width
+            result = sb.tile([P, 4, width], F32, name=f"result{c}")
+            for t in range(4):
+                diff = sb.tile([P, width], F32, name="diff", bufs=3)
+                if 4 * c + t in []:
+                    near = sb.tile([P, width], F32, name=f"near{c}{t}")
+                    nc.scalar.copy(near[:], h_acc[t][:, cols])
+                    nc.vector.tensor_tensor(diff[:], hs[t][:].indirect(n5_t[:, entries]), near[:], ALU.subtract)
+                else:
+                    far = sb.tile([P, width], F32, name="far", bufs=3)
+                    nc.scalar.activation(far[:], hs[t][:].indirect(n5_t[:, entries]), ACT.Copy)
+                    nc.vector.tensor_tensor(diff[:], far[:], hs[t][:, cols], ALU.subtract)
+                bent = sb.tile([P, width], F32, name="bent", bufs=3)
+                nc.scalar.activation(bent[:], diff[:], ACT.Tanh)
+                nc.vector.tensor_tensor(result[:, t, :], hs[t][:].indirect(n6_t[:, entries]), bent[:], ALU.mult)
+                nc.sync.dma_start(out=out_rows[:, t, cols], in_=result[:, t, :])
+            finish.append((c, cols, result))
+            if c + 1 < 2:
+                continue
+            for c, cols, result in finish:
+                woven = weave((nc.scalar.copy, nc.vector.tensor_copy,)[c], result, f"o{c}")
+                nc.vector.quantize_mx(out=o_codes[:, cols].bitcast(FP8X4), scales=o_scales[:, cols], in_=woven[:].rearrange("p j t -> p (j t)"))
+                nc.sync.dma_start(out=out_words[:, cols], in_=o_codes[:, cols])
+            finish = []
+        for q in range(4):
+            queue = nc.sync if q % 2 else nc.scalar
+            queue.dma_start(out=out_2[0, 4 * q : 4 * q + 4, :].bitcast(I32), in_=o_scales[32 * q : 32 * q + 4, :].bitcast(I32))

@@ -98,6 +98,8 @@ def tile_picked_jkeykdifknormfdif_none_po_kernel(
         nc.vector.memset(half[:], 0.5)
 
         w1w_raw = load_fp4(w1_words, "w1w_raw")
+        warm = sb.tile([P, 1], F32, name="warm")
+        nc.scalar.activation(warm[:], half[:], ACT.Abs_reciprocal_sqrt, bias=half[:])
         offs_t = load_list(offs, "offs_t")
         xw_table = load_words(x_words, "xw_table")
         load_scale_rows(xs_table, x_scales)
@@ -204,6 +206,8 @@ def tile_picked_jkeykdifknormfdif_none_po_kernel(
         for t in range(4):
             nc.scalar.activation(ys[t][:].indirect(n1_t[:]), ra[:, t, :], ACT.Copy)
             rounded(z_planes, ys, gn_t, t, [])
+        warm2 = sb.tile([P, 1], F32, name="warm2")
+        nc.scalar.activation(warm2[:], ys[3][:, 0:1], ACT.Tanh)
         z_codes, z_scales = quantize(z_planes, "z")
 
         h_acc = [psum.tile([P, S], F32, name=f"h_acc{t}", tag=f"bank_a{t}") for t in range(4)]

@@ -49,7 +49,7 @@ def tile_picked_jkeykdifknormfdif_none_po_kernel(
             return tile
 
         def load_fp4(src, name):
-            tile = sb.tile([P, 2 * S], U8, name=name, tag="fp4_raw", align_bytes=64)
+            tile = sb.tile([P, 2 * S], U8, name=name, tag="fp4_raw" if name != "w3w_raw" else name, align_bytes=64)
             nc.sync.dma_start(out=tile[:].bitcast(I32), in_=src[0].bitcast(I32))
             return tile
 
@@ -77,7 +77,7 @@ def tile_picked_jkeykdifknormfdif_none_po_kernel(
             return tile
 
         def weave(copy, planes, name):
-            woven = sb.tile([P, planes.shape[2], 4], BF16, name=name + "_woven", align_bytes=64)
+            woven = sb.tile([P, planes.shape[2], 4], BF16, name=name + "_woven", tag="held" if name == "o0" else name + "_woven", align_bytes=64)
             copy(woven[:].rearrange("p (c i) t -> p c t i", i=4), planes[:].rearrange("p t (c i) -> p c t i", i=4))
             return woven
 
@@ -101,10 +101,10 @@ def tile_picked_jkeykdifknormfdif_none_po_kernel(
         warm = sb.tile([P, 1], F32, name="warm")
         nc.scalar.activation(warm[:], half[:], ACT.Abs_reciprocal_sqrt, bias=half[:])
         offs_t = load_list(offs, "offs_t")
-        xw_table = load_words(x_words, "xw_table")
-        load_scale_rows(xs_table, x_scales)
-        load_scale_rows(w1s_raw, w1_scales)
         kidx_t = load_list(kidx, "kidx_t")
+        load_scale_rows(xs_table, x_scales)
+        xw_table = load_words(x_words, "xw_table")
+        load_scale_rows(w1s_raw, w1_scales)
         nc.sync.dma_start(out=ds_table[0:P:8, :].bitcast(I32), in_=d_scales[0].bitcast(I32))
         n2_t = load_list(n2, "n2_t")
         dw_table = load_words(d_words, "dw_table")
@@ -135,18 +135,23 @@ def tile_picked_jkeykdifknormfdif_none_po_kernel(
                 in_=dq_scales_dealt[32 * q : 32 * (q + 1) : 8, :].bitcast(I32),
             )
         dq_words = gather_codes(dw_table, kidx_t, U32, "dq_words")
-        dq_words_dealt = deal(dq_words[:].bitcast(I32), I32, 1, "dq_words_dealt", "keys_then_ra")
+        keys = []
+        for u in range(2):
+            pair = sb.tile([P, 2, P], I32, name=f"keys{u}", tag=f"keys_then_ra{u}", align_bytes=64)
+            nc.vector.tensor_copy(out=pair[:], in_=dq_words[:].bitcast(I32).rearrange("p (m t) -> p t m", t=4)[:, 2 * u : 2 * u + 2, :])
+            keys.append(pair)
         x2_scales = gather_bytes(xs_table, two_t, "x2_scales")
         x2_words = gather_codes(xw_table, two_t, U32, "x2_words")
 
         s_acc = [psum.tile([P, S], F32, name=f"s_acc{t}", tag=f"bank_b{t}") for t in range(4)]
         for t in range(4):
             nc.tensor.matmul_mx(
-                out=s_acc[t][:], lhsT=dq_words_dealt[:, P * t : P * (t + 1)].bitcast(FP8X4), lhsT_scale=ds_final[:, P * t : P * (t + 1)],
+                out=s_acc[t][:], lhsT=keys[t // 2][:, t % 2, :].bitcast(FP8X4), lhsT_scale=ds_final[:, P * t : P * (t + 1)],
                 rhs=x2_words[:].bitcast(FP8X4), rhs_scale=x2_scales[:], start=True, stop=True,
             )
 
         w2w_raw = load_fp4(w2_words, "w2w_raw")
+        w3w_raw = load_fp4(w3_words, "w3w_raw")
         load_scale_rows(w2s_raw, w2_scales)
         load_scale_rows(w3s_raw, w3_scales)
         n5_t = load_list(n5, "n5_t")
@@ -160,14 +165,13 @@ def tile_picked_jkeykdifknormfdif_none_po_kernel(
             nc.scalar.activation(less[:], ys[t][:].indirect(n2_t[:]), ACT.Copy, scale=-0.5)
             lesses.append(less)
 
-        w2w = deal(w2w_raw[:], U8, 2, "w2w")
-        w3w_raw = load_fp4(w3_words, "w3w_raw")
+        w2w = deal(w2w_raw[:], U8, 2, "w2w", "xw_table")
+        w3w = deal(w3w_raw[:], U8, 2, "w3w", "xs_table")
         w2s = deal(w2s_raw[:], U8, 1, "w2s")
         w3s = deal(w3s_raw[:], U8, 1, "w3s")
-        ra = sb.tile([P, 4, W], F32, name="ra", tag="keys_then_ra", align_bytes=64)
+        ra = [sb.tile([P, 2, W], F32, name=f"ra{u}", tag=f"keys_then_ra{u}", align_bytes=64) for u in range(2)]
         for t in range(4):
-            nc.vector.tensor_tensor(ra[:, t, :], ys[t][:].indirect(n1_t[:]), lesses[t][:], ALU.add)
-        w3w = deal(w3w_raw[:], U8, 2, "w3w")
+            nc.vector.tensor_tensor(ra[t // 2][:, t % 2, :], ys[t][:].indirect(n1_t[:]), lesses[t][:], ALU.add)
         gk16 = sb.tile([P, 4], F32, name="gk16")
         nc.vector.tensor_scalar(gk16[:], gk_t[:], 0.0625, None, ALU.mult)
 
@@ -192,23 +196,29 @@ def tile_picked_jkeykdifknormfdif_none_po_kernel(
             nc.scalar.activation(root[:], size[:], ACT.Abs_reciprocal_sqrt, bias=half[:])
             once = sb.tile([P, W], F32, name=f"once{t}")
             nc.vector.tensor_tensor(once[:], ss[t][:].indirect(n3_t[:]), root[:], ALU.mult)
-            if t in []:
-                twice = sb.tile([P, W], F32, name=f"twice{t}")
-                nc.vector.tensor_tensor(twice[:], once[:], root[:], ALU.mult)
+            if t in [0]:
+                twice = sb.tile([P, W - 128], F32, name=f"twice{t}")
+                nc.vector.tensor_tensor(twice[:], once[:, 128:], root[:, 128:], ALU.mult)
+                nc.vector.tensor_tensor(ss[t][:].indirect(n3_t[:, : 8]), once[:, :128], root[:, :128], ALU.mult)
                 late.append((t, twice))
             else:
                 nc.vector.tensor_tensor(ss[t][:].indirect(n3_t[:]), once[:], root[:], ALU.mult)
                 rounded(z2_planes, ss, gk16, t, [])
         for t, twice in late:
-            nc.scalar.activation(ss[t][:].indirect(n3_t[:]), twice[:], ACT.Copy)
+            nc.scalar.activation(ss[t][:].indirect(n3_t[:, 8 :]), twice[:], ACT.Copy)
             rounded(z2_planes, ss, gk16, t, [])
         z2_codes, z2_scales = quantize(z2_planes, "z2")
         for t in range(4):
-            nc.scalar.activation(ys[t][:].indirect(n1_t[:]), ra[:, t, :], ACT.Copy)
+            nc.scalar.activation(ys[t][:].indirect(n1_t[:]), ra[t // 2][:, t % 2, :], ACT.Copy)
             rounded(z_planes, ys, gn_t, t, [])
+        z_woven = sb.tile([P, S, 4], BF16, name="z_woven", align_bytes=64)
+        for copy, cols in ((nc.vector.tensor_copy, slice(0, 384)), (nc.scalar.copy, slice(384, S))):
+            copy(z_woven[:, cols, :].rearrange("p (c i) t -> p c t i", i=4), z_planes[:, :, cols].rearrange("p t (c i) -> p c t i", i=4))
         warm2 = sb.tile([P, 1], F32, name="warm2")
-        nc.scalar.activation(warm2[:], ys[3][:, 0:1], ACT.Tanh)
-        z_codes, z_scales = quantize(z_planes, "z")
+        nc.scalar.activation(warm2[:], z_woven[:, S - 1, 0:1], ACT.Tanh)
+        z_codes = sb.tile([P, S], I32, name="z_codes", align_bytes=64)
+        z_scales = sb.tile([P, S], U8, name="z_scales", align_bytes=64)
+        nc.vector.quantize_mx(out=z_codes[:].bitcast(FP8X4), scales=z_scales[:], in_=z_woven[:].rearrange("p j t -> p (j t)"))
 
         h_acc = [psum.tile([P, S], F32, name=f"h_acc{t}", tag=f"bank_a{t}") for t in range(4)]
         for first, ww, ws, codes, scales in ((True, w3w, w3s, z2_codes, z2_scales), (False, w2w, w2s, z_codes, z_scales)):
@@ -233,16 +243,19 @@ def tile_picked_jkeykdifknormfdif_none_po_kernel(
             start = start + width
             result = sb.tile([P, 4, width], F32, name=f"result{c}")
             for t in range(4):
-                diff = sb.tile([P, width], F32, name="diff", bufs=3)
+                if 4 * c + t == 7:
+                    diff = sb.tile([P, width], F32, name="held", tag="held", align_bytes=64)
+                else:
+                    diff = sb.tile([P, width], F32, name="diff", bufs=4)
                 if 4 * c + t in []:
                     near = sb.tile([P, width], F32, name=f"near{c}{t}")
                     nc.scalar.copy(near[:], h_acc[t][:, cols])
                     nc.vector.tensor_tensor(diff[:], hs[t][:].indirect(n5_t[:, entries]), near[:], ALU.subtract)
                 else:
-                    far = sb.tile([P, width], F32, name="far", bufs=3)
+                    far = sb.tile([P, width], F32, name="far", bufs=4)
                     nc.scalar.activation(far[:], hs[t][:].indirect(n5_t[:, entries]), ACT.Copy)
                     nc.vector.tensor_tensor(diff[:], far[:], hs[t][:, cols], ALU.subtract)
-                bent = sb.tile([P, width], F32, name="bent", bufs=3)
+                bent = sb.tile([P, width], F32, name="bent", bufs=4)
                 nc.scalar.activation(bent[:], diff[:], ACT.Tanh)
                 nc.vector.tensor_tensor(result[:, t, :], hs[t][:].indirect(n6_t[:, entries]), bent[:], ALU.mult)
                 nc.sync.dma_start(out=out_rows[:, t, cols], in_=result[:, t, :])

from contextlib import ExitStack

import concourse.mybir as mybir

F32 = mybir.dt.float32
BF16 = mybir.dt.bfloat16
I32 = mybir.dt.int32
U32 = mybir.dt.uint32
U16 = mybir.dt.uint16
U8 = mybir.dt.uint8
FP8X4 = mybir.dt.float8_e4m3fn_x4
FP4X4 = mybir.dt.float4_e2m1fn_x4
ACT = mybir.ActivationFunctionType
ALU = mybir.AluOpType

P = 128
S = 512
W = 384
FLOPS = 4 * 2 * 512 * 512 * 512


def tile_picked_jkeykdifknormfdif_none_po_kernel(
    tc, x_words, x_scales, w1_words, w1_scales, d_words, d_scales, gn, gk, w2_words, w2_scales,
    w3_words, w3_scales, offs, kidx, two, n1, n2, n3, n4, n5, n6, out_0, out_1, out_2,
):
    nc = tc.nc
    with ExitStack() as ctx:
        lists = ctx.enter_context(tc.tile_pool(name="lists", bufs=1))
        sb = ctx.enter_context(tc.tile_pool(name="sb", bufs=1))
        psum = ctx.enter_context(tc.psum_pool(name="psum", bufs=1))

        def load_list(src, name):
            tile = lists.tile([P, src.shape[1]], U16, name=name)
            nc.sync.dma_start(tile[:], src)
            return tile

        def zeroed_bytes(width, name):
            tile = sb.tile([P, width], U8, name=name, align_bytes=64)
            nc.vector.memset(tile[:].bitcast(I32), 0)
            return tile

        def load_scale_rows(tile, src):
            for q in range(4):
                nc.sync.dma_start(out=tile[32 * q : 32 * q + 4, :].bitcast(I32), in_=src[0, 4 * q : 4 * q + 4, :].bitcast(I32))

        def load_words(src, name):
            tile = sb.tile([P, src.shape[2]], I32, name=name, align_bytes=64)
            nc.sync.dma_start(out=tile[:], in_=src[0].rearrange("p n t -> p (n t)").bitcast(I32))
            return tile

        def load_fp4(src, name):
            tile = sb.tile([P, 2 * S], U8, name=name, tag="fp4_raw" if name != "w3w_raw" else name, align_bytes=64)
            nc.sync.dma_start(out=tile[:].bitcast(I32), in_=src[0].bitcast(I32))
            return tile

        def load_gain(src, name):
            tile = sb.tile([P, 4], F32, name=name)
            nc.sync.dma_start(out=tile[:], in_=src.rearrange("(p t) o -> p (t o)", t=4))
            return tile

        def deal(src, dtype, width, name, tag=None, engine=nc.vector):
            tile = sb.tile([P, S * width], dtype, name=name, tag=tag or name, align_bytes=64)
            engine.tensor_copy(
                out=tile[:].rearrange("p (t m b) -> p t m b", t=4, b=width),
                in_=src.rearrange("p (m t b) -> p t m b", t=4, b=width),
            )
            return tile

        def gather_codes(table, offsets, dtype, name):
            tile = sb.tile([P, S], dtype, name=name, align_bytes=64)
            nc.vector.tensor_copy(tile[:], table[:].bitcast(dtype).indirect(offsets[:]))
            return tile

        def gather_bytes(table, offsets, name):
            tile = sb.tile([P, S], U8, name=name, align_bytes=64)
            nc.vector.tensor_copy(tile[:], table[:].indirect(offsets[:]))
            return tile

        def weave(copy, planes, name):
            woven = sb.tile([P, planes.shape[2], 4], BF16, name=name + "_woven", tag="held" if name == "o0" else name + "_woven", align_bytes=64)
            copy(woven[:].rearrange("p (c i) t -> p c t i", i=4), planes[:].rearrange("p t (c i) -> p c t i", i=4))
            return woven

        def quantize(planes, name):
            woven = weave(nc.vector.tensor_copy, planes, name)
            codes = sb.tile([P, S], I32, name=name + "_codes", align_bytes=64)
            scales = sb.tile([P, S], U8, name=name + "_scales", align_bytes=64)
            nc.vector.quantize_mx(out=codes[:].bitcast(FP8X4), scales=scales[:], in_=woven[:].rearrange("p j t -> p (j t)"))
            return codes, scales

        xs_table = zeroed_bytes(1024, "xs_table")
        w1s_raw = zeroed_bytes(S, "w1s_raw")
        ds_table = zeroed_bytes(2048, "ds_table")
        ds_final = zeroed_bytes(S, "ds_final")
        w2s_raw = zeroed_bytes(S, "w2s_raw")
        w3s_raw = zeroed_bytes(S, "w3s_raw")
        half = sb.tile([P, 1], F32, name="half")
        nc.vector.memset(half[:], 0.5)

        w1w_raw = load_fp4(w1_words, "w1w_raw")
        warm = sb.tile([P, 1], F32, name="warm")
        nc.scalar.activation(warm[:], half[:], ACT.Abs_reciprocal_sqrt, bias=half[:])
        offs_t = load_list(offs, "offs_t")
        kidx_t = load_list(kidx, "kidx_t")
        load_scale_rows(xs_table, x_scales)
        xw_table = load_words(x_words, "xw_table")
        load_scale_rows(w1s_raw, w1_scales)
        nc.sync.dma_start(out=ds_table[0:P:8, :].bitcast(I32), in_=d_scales[0].bitcast(I32))
        n2_t = load_list(n2, "n2_t")
        dw_table = load_words(d_words, "dw_table")
        two_t = load_list(two, "two_t")
        n1_t = load_list(n1, "n1_t")
        n4_t = load_list(n4, "n4_t")
        n3_t = load_list(n3, "n3_t")
        gn_t = load_gain(gn, "gn_t")
        gk_t = load_gain(gk, "gk_t")

        xq_scales = gather_bytes(xs_table, offs_t, "xq_scales")
        xq_words = gather_codes(xw_table, offs_t, U32, "xq_words")
        w1w = deal(w1w_raw[:], U8, 2, "w1w")
        w1s = deal(w1s_raw[:], U8, 1, "w1s")

        y_acc = [psum.tile([P, S], F32, name=f"y_acc{t}", tag=f"bank_a{t}") for t in range(4)]
        for t in range(4):
            nc.tensor.matmul_mx(
                out=y_acc[t][:], lhsT=w1w[:, 256 * t : 256 * (t + 1)].bitcast(FP4X4), lhsT_scale=w1s[:, P * t : P * (t + 1)],
                rhs=xq_words[:].bitcast(FP8X4), rhs_scale=xq_scales[:], start=True, stop=True,
            )

        dq_scales = gather_bytes(ds_table, kidx_t, "dq_scales")
        dq_scales_dealt = deal(dq_scales[:], U8, 1, "dq_scales_dealt")
        for q in range(4):
            nc.sync.dma_start(
                out=ds_final[32 * q : 32 * q + 4, :].bitcast(I32),
                in_=dq_scales_dealt[32 * q : 32 * (q + 1) : 8, :].bitcast(I32),
            )
        dq_words = gather_codes(dw_table, kidx_t, U32, "dq_words")
        keys = []
        for u in range(2):
            pair = sb.tile([P, 2, P], I32, name=f"keys{u}", tag=f"keys_then_ra{u}", align_bytes=64)
            nc.vector.tensor_copy(out=pair[:], in_=dq_words[:].bitcast(I32).rearrange("p (m t) -> p t m", t=4)[:, 2 * u : 2 * u + 2, :])
            keys.append(pair)
        x2_scales = gather_bytes(xs_table, two_t, "x2_scales")
        x2_words = gather_codes(xw_table, two_t, U32, "x2_words")

        s_acc = [psum.tile([P, S], F32, name=f"s_acc{t}", tag=f"bank_b{t}") for t in range(4)]
        for t in range(4):
            nc.tensor.matmul_mx(
                out=s_acc[t][:], lhsT=keys[t // 2][:, t % 2, :].bitcast(FP8X4), lhsT_scale=ds_final[:, P * t : P * (t + 1)],
                rhs=x2_words[:].bitcast(FP8X4), rhs_scale=x2_scales[:], start=True, stop=True,
            )

        w2w_raw = load_fp4(w2_words, "w2w_raw")
        w3w_raw = load_fp4(w3_words, "w3w_raw")
        load_scale_rows(w2s_raw, w2_scales)
        load_scale_rows(w3s_raw, w3_scales)
        n5_t = load_list(n5, "n5_t")
        n6_t = load_list(n6, "n6_t")

        ys = [sb.tile([P, S], F32, name=f"y{t}") for t in range(4)]
        lesses = []
        for t in range(4):
            (nc.vector.tensor_copy if t in [] else nc.scalar.copy)(ys[t][:], y_acc[t][:])
            less = sb.tile([P, W], F32, name=f"less{t}")
            nc.scalar.activation(less[:], ys[t][:].indirect(n2_t[:]), ACT.Copy, scale=-0.5)
            lesses.append(less)

        w2w = deal(w2w_raw[:], U8, 2, "w2w", "xw_table")
        w3w = deal(w3w_raw[:], U8, 2, "w3w", "xs_table")
        w2s = deal(w2s_raw[:], U8, 1, "w2s")
        w3s = deal(w3s_raw[:], U8, 1, "w3s")
        ra = [sb.tile([P, 2, W], F32, name=f"ra{u}", tag=f"keys_then_ra{u}", align_bytes=64) for u in range(2)]
        for t in range(4):
            nc.vector.tensor_tensor(ra[t // 2][:, t % 2, :], ys[t][:].indirect(n1_t[:]), lesses[t][:], ALU.add)
        gk16 = sb.tile([P, 4], F32, name="gk16")
        nc.vector.tensor_scalar(gk16[:], gk_t[:], 0.0625, None, ALU.mult)

        z_planes = sb.tile([P, 4, S], BF16, name="z_planes")
        z2_planes = sb.tile([P, 4, S], BF16, name="z2_planes")
        late = []

        def rounded(planes, tiles, gain, t, on_scalar):
            if t in on_scalar:
                nc.scalar.activation(planes[:, t, :], tiles[t][:], ACT.Copy, scale=gain[:, t : t + 1])
            else:
                nc.vector.tensor_scalar(planes[:, t, :], tiles[t][:], gain[:, t : t + 1], None, ALU.mult)

        ss = [sb.tile([P, S], F32, name=f"s{t}") for t in range(4)]
        for t in range(4):
            (nc.vector.tensor_copy if t in [] else nc.scalar.copy)(ss[t][:], s_acc[t][:])
            pa2 = sb.tile([P, W], F32, name=f"pa2_{t}")
            nc.scalar.activation(pa2[:], ss[t][:].indirect(n4_t[:]), ACT.Copy)
            size = sb.tile([P, W], F32, name=f"size{t}")
            nc.scalar.activation(size[:], pa2[:], ACT.Abs, scale=0.0625)
            root = sb.tile([P, W], F32, name=f"root{t}")
            nc.scalar.activation(root[:], size[:], ACT.Abs_reciprocal_sqrt, bias=half[:])
            once = sb.tile([P, W], F32, name=f"once{t}")
            nc.vector.tensor_tensor(once[:], ss[t][:].indirect(n3_t[:]), root[:], ALU.mult)
            if t in [0]:
                twice = sb.tile([P, W - 128], F32, name=f"twice{t}")
                nc.vector.tensor_tensor(twice[:], once[:, 128:], root[:, 128:], ALU.mult)
                nc.vector.tensor_tensor(ss[t][:].indirect(n3_t[:, : 8]), once[:, :128], root[:, :128], ALU.mult)
                late.append((t, twice))
            else:
                nc.vector.tensor_tensor(ss[t][:].indirect(n3_t[:]), once[:], root[:], ALU.mult)
                rounded(z2_planes, ss, gk16, t, [])
        for t, twice in late:
            nc.scalar.activation(ss[t][:].indirect(n3_t[:, 8 :]), twice[:], ACT.Copy)
            rounded(z2_planes, ss, gk16, t, [])
        z2_codes, z2_scales = quantize(z2_planes, "z2")
        for t in range(4):
            nc.scalar.activation(ys[t][:].indirect(n1_t[:]), ra[t // 2][:, t % 2, :], ACT.Copy)
            rounded(z_planes, ys, gn_t, t, [])
        z_woven = sb.tile([P, S, 4], BF16, name="z_woven", align_bytes=64)
        for copy, cols in ((nc.vector.tensor_copy, slice(0, 384)), (nc.scalar.copy, slice(384, S))):
            copy(z_woven[:, cols, :].rearrange("p (c i) t -> p c t i", i=4), z_planes[:, :, cols].rearrange("p t (c i) -> p c t i", i=4))
        warm2 = sb.tile([P, 1], F32, name="warm2")
        nc.scalar.activation(warm2[:], z_woven[:, S - 1, 0:1], ACT.Tanh)
        z_codes = sb.tile([P, S], I32, name="z_codes", align_bytes=64)
        z_scales = sb.tile([P, S], U8, name="z_scales", align_bytes=64)
        nc.vector.quantize_mx(out=z_codes[:].bitcast(FP8X4), scales=z_scales[:], in_=z_woven[:].rearrange("p j t -> p (j t)"))

        h_acc = [psum.tile([P, S], F32, name=f"h_acc{t}", tag=f"bank_a{t}") for t in range(4)]
        for first, ww, ws, codes, scales in ((True, w3w, w3s, z2_codes, z2_scales), (False, w2w, w2s, z_codes, z_scales)):
            for t in range(4):
                nc.tensor.matmul_mx(
                    out=h_acc[t][:], lhsT=ww[:, 256 * t : 256 * (t + 1)].bitcast(FP4X4), lhsT_scale=ws[:, P * t : P * (t + 1)],
                    rhs=codes[:].bitcast(FP8X4), rhs_scale=scales[:], start=first, stop=not first,
                )

        hs = [sb.tile([P, S], F32, name=f"h{t}") for t in range(4)]
        for t in range(4):
            (nc.scalar.copy if t in [0] else nc.vector.tensor_copy)(hs[t][:], h_acc[t][:])
        out_rows = out_0.rearrange("(p t) j -> p t j", t=4)
        out_words = out_1[0].rearrange("p n t -> p (n t)").bitcast(I32)
        o_codes = sb.tile([P, S], I32, name="o_codes", align_bytes=64)
        o_scales = sb.tile([P, S], U8, name="o_scales", align_bytes=64)
        start = 0
        finish = []
        for c, width in enumerate([256,256]):
            cols = slice(start, start + width)
            entries = slice(start // 16, (start + width) // 16)
            start = start + width
            result = sb.tile([P, 4, width], F32, name=f"result{c}")
            for t in range(4):
                if 4 * c + t == 7:
                    diff = sb.tile([P, width], F32, name="held", tag="held", align_bytes=64)
                else:
                    diff = sb.tile([P, width], F32, name="diff", bufs=4)
                if 4 * c + t in []:
                    near = sb.tile([P, width], F32, name=f"near{c}{t}")
                    nc.scalar.copy(near[:], h_acc[t][:, cols])
                    nc.vector.tensor_tensor(diff[:], hs[t][:].indirect(n5_t[:, entries]), near[:], ALU.subtract)
                else:
                    far = sb.tile([P, width], F32, name="far", bufs=4)
                    nc.scalar.activation(far[:], hs[t][:].indirect(n5_t[:, entries]), ACT.Copy)
                    nc.vector.tensor_tensor(diff[:], far[:], hs[t][:, cols], ALU.subtract)
                bent = sb.tile([P, width], F32, name="bent", bufs=4)
                nc.scalar.activation(bent[:], diff[:], ACT.Tanh)
                nc.vector.tensor_tensor(result[:, t, :], hs[t][:].indirect(n6_t[:, entries]), bent[:], ALU.mult)
                nc.sync.dma_start(out=out_rows[:, t, cols], in_=result[:, t, :])
            finish.append((c, cols, result))
            if c + 1 < 2:
                continue
            for c, cols, result in finish:
                woven = weave((nc.scalar.copy, nc.vector.tensor_copy,)[c], result, f"o{c}")
                nc.vector.quantize_mx(out=o_codes[:, cols].bitcast(FP8X4), scales=o_scales[:, cols], in_=woven[:].rearrange("p j t -> p (j t)"))
                nc.sync.dma_start(out=out_words[:, cols], in_=o_codes[:, cols])
            finish = []
        for q in range(4):
            queue = nc.sync if q % 2 else nc.scalar
            queue.dma_start(out=out_2[0, 4 * q : 4 * q + 4, :].bitcast(I32), in_=o_scales[32 * q : 32 * q + 4, :].bitcast(I32))
